import numpy as np, ml_dtypes
CORES = [2,10,18,26,34,42,130,138,146]
N = 9
TK = 512
D = 128 * N
def setup_inputs(rng):
    return {"x": (rng.standard_normal((N, 128, TK), dtype=np.float32) + 2 * rng.standard_normal((N, 1, TK), dtype=np.float32)).astype(ml_dtypes.bfloat16)}
def reference(x):
    X = x.astype(np.float64)
    m = X.sum(axis=(0, 1)) / D
    s = ((X - m) ** 2).sum(axis=(0, 1)) / D
    return {"y": (X - m).astype(np.float32), "m": np.broadcast_to(m.astype(np.float32), (N, 1, TK)), "s": np.broadcast_to(s.astype(np.float32), (N, 1, TK))}

@@ -1,0 +1,150 @@
+from concourse.bass import DstId, RemoteDMATransfer
+from concourse.mybir import dt, AluOpType
+
+N = 9
+TK = 512
+D = 128 * N
+NB = 4
+K = N * 3 * NB
+
+SCRATCH = {
+    "xs": ("sbuf", [128, TK], "bfloat16"),
+    "xq": ("sbuf", [128, TK], "float32"),
+    "ysb": ("sbuf", [128, TK], "float32"),
+    "R": ("sbuf", [128, N * 24], "bfloat16"),
+    "onesb": ("sbuf", [128, 8], "bfloat16"),
+    "onesf": ("sbuf", [128, 4], "float32"),
+    "invd": ("sbuf", [128, 8], "float32"),
+    "sc": ("sbuf", [128, 8], "float32"),
+    "r1": ("sbuf", [128, 8], "float32"),
+    "ia": ("sbuf", [128, 129], "bfloat16"),
+    "ident": ("sbuf", [128, 128], "bfloat16"),
+    "w": ("sbuf", [128, 896], "bfloat16"),
+    "sel": ("sbuf", [128, TK], "bfloat16"),
+    "rt1": ("sbuf", [128, 128], "bfloat16"),
+    "rt2": ("sbuf", [128, 128], "bfloat16"),
+    "msb": ("sbuf", [128, 4], "float32"),
+    "msq": ("sbuf", [128, 4], "float32"),
+    "ssb": ("sbuf", [128, 4], "float32"),
+    "di": ("dram", [129, 128], "bfloat16"),
+    "ps": ("psum", [128, 512], "float32"),
+    "pt1": ("psum", [128, 512], "float32"),
+    "pt2": ("psum", [128, 512], "float32"),
+    "pm0": ("psum", [128, 512], "float32"),
+    "pm1": ("psum", [128, 512], "float32"),
+    "pm2": ("psum", [128, 512], "float32"),
+    "pm3": ("psum", [128, 512], "float32"),
+}
+SEMAPHORES = ["ld", "c0", "c1", "c2", "id1", "id2", "sl", "sq0", "sq1", "sq2", "sq3", "st", "p1", "p2", "p3", "p4",
+              "arr", "sent", "t1", "t2", "r1s", "r2s", "mb0", "mb1", "mb2", "mb3", "ms", "yd", "m1", "m2", "m3",
+              "outy", "outm", "outs"]
+
+
+def _links(topo, a, b):
+    if topo.mates(a, b) or topo.same_plane(a, b):
+        return 1
+    return 2
+
+
+def rank_program(g, core, T, topo):
+    rank = T.rank_of(core)
+    if rank is None:
+        return
+    S = T.sem
+    pe, ve, sy, sa = g.tensor, g.vector, g.sync, g.scalar
+    R = T.R
+    slot = R[:, 24 * rank:24 * rank + 24]
+    hi, mid, lo = [R[:, 24 * rank + 8 * i:24 * rank + 8 * i + 8] for i in range(3)]
+
+    sy.dma_start(T.xs[:], T.x[:]).then_inc(S.ld, 16)
+
+    ve.memset(T.onesb[:], 1.0).then_inc(S.c0, 1)
+    ve.memset(T.onesf[:], 1.0).then_inc(S.c0, 1)
+    ve.memset(T.invd[:], 1.0 / D).then_inc(S.c0, 1)
+    ve.memset(T.ia[:, 0:1], 1.0).then_inc(S.c1, 1)
+    ve.memset(T.ia[:, 1:129], 0.0).then_inc(S.c1, 1)
+    ve.memset(T.w[0:27, 0:384], 0.0).then_inc(S.c2, 1)
+    ve.memset(T.w[0:27, 384:512], 1.0).then_inc(S.c2, 1)
+    ve.memset(T.w[0:27, 512:896], 0.0).then_inc(S.c2, 1)
+    sa.wait_ge(S.c1, 2)
+    sa.dma_start(T.di[:], T.ia[:]).then_inc(S.id1, 16)
+    sa.wait_ge(S.c2, 3)
+    for b in range(NB):
+        sa.dma_start(T.sel[b:K:NB, :], T.w[0:27, 384 - 128 * b:896 - 128 * b]).then_inc(S.sl, 16)
+    sa.wait_ge(S.id1, 16)
+    sa.dma_start(T.ident[:], T.di[0:128, :]).then_inc(S.id2, 16)
+
+    pe.wait_ge(S.ld, 16)
+    pe.wait_ge(S.c0, 3)
+    for b in range(NB):
+        pe.matmul(T.ps[:, 2 * b:2 * b + 1], T.xs[:, b::NB], T.onesb[:, 0:1], True, True).then_inc(S.st, 1)
+    ve.wait_ge(S.ld, 16)
+    for b in range(NB):
+        ve.tensor_tensor(T.xq[:, 128 * b:128 * b + 128], T.xs[:, b::NB], T.xs[:, b::NB],
+                         AluOpType.mult).then_inc(S["sq%d" % b], 1)
+        pe.wait_ge(S["sq%d" % b], 1)
+        pe.matmul(T.ps[:, 2 * b + 1:2 * b + 2], T.xq[:, 128 * b:128 * b + 128], T.onesf[:, 0:1],
+                  True, True).then_inc(S.st, 1)
+
+    ve.wait_ge(S.st, 8)
+    ve.wait_ge(S.c0, 3)
+    ve.tensor_tensor(T.sc[:], T.ps[:, 0:8], T.invd[:], AluOpType.mult).then_inc(S.p1, 1)
+    ve.tensor_tensor(hi, T.ps[:, 0:8], T.invd[:], AluOpType.mult).then_inc(S.p1, 1)
+    ve.wait_ge(S.p1, 2)
+    ve.tensor_tensor(T.r1[:], T.sc[:], hi, AluOpType.subtract).then_inc(S.p2, 1)
+    ve.wait_ge(S.p2, 1)
+    ve.tensor_copy(mid, T.r1[:]).then_inc(S.p3, 1)
+    ve.wait_ge(S.p3, 1)
+    ve.tensor_tensor(lo, T.r1[:], mid, AluOpType.subtract).then_inc(S.p4, 1)
+
+    peers = sorted([c for c in T.cores if c != core], key=lambda c: -_links(topo, core, c))
+    mask = topo.mask(core, peers[0])
+    for c in peers:
+        mask &= topo.mask(core, c)
+    eng = bin(mask).count("1")
+    ids = []
+    for c in peers:
+        rid, pid = topo.addr(c, core)
+        ids.append(DstId(rid=rid, pnc=pid))
+    g.wait_ge(S.p4, 1)
+    g.remote_dma_fused([RemoteDMATransfer(dst_ids=ids, dma_engine_mask=mask, remote_sem=S.arr,
+                                          srcs=[slot], dsts=[slot for _ in peers])], local_sem=S.sent)
+
+    pe.wait_ge(S.p4, 1)
+    pe.wait_ge(S.id2, 16)
+    pe.wait_ge(S.arr, eng * (N - 1))
+    pe.matmul(T.pt1[0:K, 0:128], R[:, 0:2 * K:2], T.ident[:], True, True).then_inc(S.t1, 1)
+    pe.matmul(T.pt2[0:K, 0:128], R[:, 1:2 * K:2], T.ident[:], True, True).then_inc(S.t2, 1)
+    ve.wait_ge(S.t1, 1)
+    ve.tensor_copy(T.rt1[0:K, :], T.pt1[0:K, 0:128]).then_inc(S.r1s, 1)
+    ve.wait_ge(S.t2, 1)
+    ve.tensor_copy(T.rt2[0:K, :], T.pt2[0:K, 0:128]).then_inc(S.r2s, 1)
+
+    pe.wait_ge(S.r1s, 1)
+    pe.wait_ge(S.sl, 16 * NB)
+    for b in range(NB):
+        pm = T["pm%d" % b]
+        pe.matmul(pm[:, 0:128], T.sel[0:K, 128 * b:128 * b + 128], T.rt1[0:K, :], True, True).then_inc(S["mb%d" % b], 1)
+        ve.wait_ge(S["mb%d" % b], 1)
+        ve.tensor_tensor(T.ysb[:, b::NB], T.xs[:, b::NB], pm[:, 0:128], AluOpType.subtract).then_inc(S.yd, 1)
+    sy.wait_ge(S.yd, NB)
+    sy.dma_start(T.y[:], T.ysb[:]).then_inc(S.outy, 16)
+
+    pe.matmul(T.ps[:, 8:12], T.rt1[0:K, :], T.sel[0:K, 0:TK:128], True, True).then_inc(S.ms, 1)
+    pe.wait_ge(S.r2s, 1)
+    pe.matmul(T.ps[:, 12:16], T.rt2[0:K, :], T.sel[0:K, 0:TK:128], True, True).then_inc(S.ms, 1)
+    ve.wait_ge(S.ms, 2)
+    ve.tensor_copy(T.msb[:], T.ps[:, 8:12]).then_inc(S.m1, 1)
+    sa.wait_ge(S.m1, 1)
+    sa.dma_start(T.m[:], T.msb[:]).then_inc(S.outm, 16)
+    ve.wait_ge(S.m1, 1)
+    ve.tensor_tensor(T.msq[:], T.ps[:, 8:12], T.msb[:], AluOpType.mult).then_inc(S.m2, 1)
+    ve.wait_ge(S.m2, 1)
+    ve.tensor_tensor(T.ssb[:], T.ps[:, 12:16], T.msq[:], AluOpType.subtract).then_inc(S.m3, 1)
+    sa.wait_ge(S.m3, 1)
+    sa.dma_start(T.s[:], T.ssb[:]).then_inc(S.outs, 16)
+
+    g.wait_ge(S.sent, eng)
+    g.wait_ge(S.outy, 16)
+    g.wait_ge(S.outm, 16)
+    g.wait_ge(S.outs, 16)

@@ -35,15 +35,20 @@ SCRATCH = {
     "pm2": ("psum", [128, 512], "float32"),
     "pm3": ("psum", [128, 512], "float32"),
 }
-SEMAPHORES = ["ld", "c0", "c1", "c2", "id1", "id2", "sl", "sq0", "sq1", "sq2", "sq3", "st", "p1", "p2", "p3", "p4",
+SEMAPHORES = ["ld", "c0", "c1", "c2", "id1", "id2", "sl", "sq0", "sq1", "sq2", "sq3", "st", "p1", "p2", "p4",
               "arr", "sent", "t1", "t2", "r1s", "r2s", "mb0", "mb1", "mb2", "mb3", "ms", "yd", "m1", "m2", "m3",
               "outy", "outm", "outs"]
 
 
-def _links(topo, a, b):
-    if topo.mates(a, b) or topo.same_plane(a, b):
-        return 1
-    return 2
+def _order(topo, cores, core):
+    mine = [c for c in cores if c == core or topo.same_plane(c, core)]
+    other = [c for c in cores if c not in mine]
+    i = mine.index(core)
+    near = [mine[(i + s) % len(mine)] for s in range(1, len(mine))]
+    mate = [c for c in other if topo.mates(core, c)]
+    j = other.index(mate[0]) if mate else i
+    far = [other[(j + 1 + k) % len(other)] for k in range(len(other))]
+    return [c for c in far if c not in mate] + mate + near
 
 
 def rank_program(g, core, T, topo):
@@ -52,17 +57,18 @@ def rank_program(g, core, T, topo):
         return
     S = T.sem
     pe, ve, sy, sa = g.tensor, g.vector, g.sync, g.scalar
+    mult, sub = AluOpType.mult, AluOpType.subtract
     R = T.R
     slot = R[:, 24 * rank:24 * rank + 24]
     hi, mid, lo = [R[:, 24 * rank + 8 * i:24 * rank + 8 * i + 8] for i in range(3)]
 
     sy.dma_start(T.xs[:], T.x[:]).then_inc(S.ld, 16)
 
+    ve.memset(T.ia[:, 0:1], 1.0).then_inc(S.c1, 1)
+    ve.memset(T.ia[:, 1:129], 0.0).then_inc(S.c1, 1)
     ve.memset(T.onesb[:], 1.0).then_inc(S.c0, 1)
     ve.memset(T.onesf[:], 1.0).then_inc(S.c0, 1)
     ve.memset(T.invd[:], 1.0 / D).then_inc(S.c0, 1)
-    ve.memset(T.ia[:, 0:1], 1.0).then_inc(S.c1, 1)
-    ve.memset(T.ia[:, 1:129], 0.0).then_inc(S.c1, 1)
     ve.memset(T.w[0:27, 0:384], 0.0).then_inc(S.c2, 1)
     ve.memset(T.w[0:27, 384:512], 1.0).then_inc(S.c2, 1)
     ve.memset(T.w[0:27, 512:896], 0.0).then_inc(S.c2, 1)
@@ -80,24 +86,22 @@ def rank_program(g, core, T, topo):
         pe.matmul(T.ps[:, 2 * b:2 * b + 1], T.xs[:, b::NB], T.onesb[:, 0:1], True, True).then_inc(S.st, 1)
     ve.wait_ge(S.ld, 16)
     for b in range(NB):
-        ve.tensor_tensor(T.xq[:, 128 * b:128 * b + 128], T.xs[:, b::NB], T.xs[:, b::NB],
-                         AluOpType.mult).then_inc(S["sq%d" % b], 1)
+        ve.tensor_tensor(T.xq[:, 128 * b:128 * b + 128], T.xs[:, b::NB], T.xs[:, b::NB], mult).then_inc(S["sq%d" % b], 1)
         pe.wait_ge(S["sq%d" % b], 1)
         pe.matmul(T.ps[:, 2 * b + 1:2 * b + 2], T.xq[:, 128 * b:128 * b + 128], T.onesf[:, 0:1],
                   True, True).then_inc(S.st, 1)
 
     ve.wait_ge(S.st, 8)
     ve.wait_ge(S.c0, 3)
-    ve.tensor_tensor(T.sc[:], T.ps[:, 0:8], T.invd[:], AluOpType.mult).then_inc(S.p1, 1)
-    ve.tensor_tensor(hi, T.ps[:, 0:8], T.invd[:], AluOpType.mult).then_inc(S.p1, 1)
+    ve.tensor_tensor(T.sc[:], T.ps[:, 0:8], T.invd[:], mult).then_inc(S.p1, 1)
+    ve.tensor_tensor(hi, T.ps[:, 0:8], T.invd[:], mult).then_inc(S.p1, 1)
     ve.wait_ge(S.p1, 2)
-    ve.tensor_tensor(T.r1[:], T.sc[:], hi, AluOpType.subtract).then_inc(S.p2, 1)
-    ve.wait_ge(S.p2, 1)
-    ve.tensor_copy(mid, T.r1[:]).then_inc(S.p3, 1)
-    ve.wait_ge(S.p3, 1)
-    ve.tensor_tensor(lo, T.r1[:], mid, AluOpType.subtract).then_inc(S.p4, 1)
+    ve.tensor_tensor(T.r1[:], T.sc[:], hi, sub).then_inc(S.p2, 1)
+    ve.tensor_tensor(mid, T.sc[:], hi, sub).then_inc(S.p2, 1)
+    ve.wait_ge(S.p2, 2)
+    ve.tensor_tensor(lo, T.r1[:], mid, sub).then_inc(S.p4, 1)
 
-    peers = sorted([c for c in T.cores if c != core], key=lambda c: -_links(topo, core, c))
+    peers = _order(topo, T.cores, core)
     mask = topo.mask(core, peers[0])
     for c in peers:
         mask &= topo.mask(core, c)
@@ -126,7 +130,7 @@ def rank_program(g, core, T, topo):
         pm = T["pm%d" % b]
         pe.matmul(pm[:, 0:128], T.sel[0:K, 128 * b:128 * b + 128], T.rt1[0:K, :], True, True).then_inc(S["mb%d" % b], 1)
         ve.wait_ge(S["mb%d" % b], 1)
-        ve.tensor_tensor(T.ysb[:, b::NB], T.xs[:, b::NB], pm[:, 0:128], AluOpType.subtract).then_inc(S.yd, 1)
+        ve.tensor_tensor(T.ysb[:, b::NB], T.xs[:, b::NB], pm[:, 0:128], sub).then_inc(S.yd, 1)
     sy.wait_ge(S.yd, NB)
     sy.dma_start(T.y[:], T.ysb[:]).then_inc(S.outy, 16)
 
@@ -138,9 +142,9 @@ def rank_program(g, core, T, topo):
     sa.wait_ge(S.m1, 1)
     sa.dma_start(T.m[:], T.msb[:]).then_inc(S.outm, 16)
     ve.wait_ge(S.m1, 1)
-    ve.tensor_tensor(T.msq[:], T.ps[:, 8:12], T.msb[:], AluOpType.mult).then_inc(S.m2, 1)
+    ve.tensor_tensor(T.msq[:], T.ps[:, 8:12], T.msb[:], mult).then_inc(S.m2, 1)
     ve.wait_ge(S.m2, 1)
-    ve.tensor_tensor(T.ssb[:], T.ps[:, 12:16], T.msq[:], AluOpType.subtract).then_inc(S.m3, 1)
+    ve.tensor_tensor(T.ssb[:], T.ps[:, 12:16], T.msq[:], sub).then_inc(S.m3, 1)
     sa.wait_ge(S.m3, 1)
     sa.dma_start(T.s[:], T.ssb[:]).then_inc(S.outs, 16)
 

@@ -5,18 +5,19 @@ N = 9
 TK = 512
 D = 128 * N
 NB = 4
-K = N * 3 * NB
+NP = 2
+SW = NP * 2 * NB
+K = N * NP * NB
 
 SCRATCH = {
     "xs": ("sbuf", [128, TK], "bfloat16"),
     "xq": ("sbuf", [128, TK], "float32"),
     "ysb": ("sbuf", [128, TK], "float32"),
-    "R": ("sbuf", [128, N * 24], "bfloat16"),
+    "R": ("sbuf", [128, N * SW], "bfloat16"),
     "onesb": ("sbuf", [128, 8], "bfloat16"),
     "onesf": ("sbuf", [128, 4], "float32"),
     "invd": ("sbuf", [128, 8], "float32"),
     "sc": ("sbuf", [128, 8], "float32"),
-    "r1": ("sbuf", [128, 8], "float32"),
     "ia": ("sbuf", [128, 129], "bfloat16"),
     "ident": ("sbuf", [128, 128], "bfloat16"),
     "w": ("sbuf", [128, 896], "bfloat16"),
@@ -28,6 +29,7 @@ SCRATCH = {
     "ssb": ("sbuf", [128, 4], "float32"),
     "di": ("dram", [129, 128], "bfloat16"),
     "ps": ("psum", [128, 512], "float32"),
+    "pq": ("psum", [128, 512], "float32"),
     "pt1": ("psum", [128, 512], "float32"),
     "pt2": ("psum", [128, 512], "float32"),
     "pm0": ("psum", [128, 512], "float32"),
@@ -35,8 +37,8 @@ SCRATCH = {
     "pm2": ("psum", [128, 512], "float32"),
     "pm3": ("psum", [128, 512], "float32"),
 }
-SEMAPHORES = ["ld", "c0", "c1", "c2", "id1", "id2", "sl", "sq0", "sq1", "sq2", "sq3", "st", "p1", "p2", "p4",
-              "arr", "sent", "t1", "t2", "r1s", "r2s", "mb0", "mb1", "mb2", "mb3", "ms", "yd", "m1", "m2", "m3",
+SEMAPHORES = ["ld", "c0", "c1", "c2", "id1", "id2", "sl", "sq0", "sq1", "sq2", "sq3", "st", "p1", "p4",
+              "arr", "sent", "t1", "t2", "r1s", "r2s", "mb0", "mb1", "mb2", "mb3", "ms1", "ms2", "yd", "m1", "m2", "m3",
               "outy", "outm", "outs"]
 
 
@@ -59,8 +61,8 @@ def rank_program(g, core, T, topo):
     pe, ve, sy, sa = g.tensor, g.vector, g.sync, g.scalar
     mult, sub = AluOpType.mult, AluOpType.subtract
     R = T.R
-    slot = R[:, 24 * rank:24 * rank + 24]
-    hi, mid, lo = [R[:, 24 * rank + 8 * i:24 * rank + 8 * i + 8] for i in range(3)]
+    slot = R[:, SW * rank:SW * rank + SW]
+    hi, mid = [R[:, SW * rank + 8 * i:SW * rank + 8 * i + 8] for i in range(NP)]
 
     sy.dma_start(T.xs[:], T.x[:]).then_inc(S.ld, 16)
 
@@ -69,14 +71,14 @@ def rank_program(g, core, T, topo):
     ve.memset(T.onesb[:], 1.0).then_inc(S.c0, 1)
     ve.memset(T.onesf[:], 1.0).then_inc(S.c0, 1)
     ve.memset(T.invd[:], 1.0 / D).then_inc(S.c0, 1)
-    ve.memset(T.w[0:27, 0:384], 0.0).then_inc(S.c2, 1)
-    ve.memset(T.w[0:27, 384:512], 1.0).then_inc(S.c2, 1)
-    ve.memset(T.w[0:27, 512:896], 0.0).then_inc(S.c2, 1)
+    ve.memset(T.w[0:K // NB, 0:384], 0.0).then_inc(S.c2, 1)
+    ve.memset(T.w[0:K // NB, 384:512], 1.0).then_inc(S.c2, 1)
+    ve.memset(T.w[0:K // NB, 512:896], 0.0).then_inc(S.c2, 1)
     sa.wait_ge(S.c1, 2)
     sa.dma_start(T.di[:], T.ia[:]).then_inc(S.id1, 16)
     sa.wait_ge(S.c2, 3)
     for b in range(NB):
-        sa.dma_start(T.sel[b:K:NB, :], T.w[0:27, 384 - 128 * b:896 - 128 * b]).then_inc(S.sl, 16)
+        sa.dma_start(T.sel[b:K:NB, :], T.w[0:K // NB, 384 - 128 * b:896 - 128 * b]).then_inc(S.sl, 16)
     sa.wait_ge(S.id1, 16)
     sa.dma_start(T.ident[:], T.di[0:128, :]).then_inc(S.id2, 16)
 
@@ -96,10 +98,7 @@ def rank_program(g, core, T, topo):
     ve.tensor_tensor(T.sc[:], T.ps[:, 0:8], T.invd[:], mult).then_inc(S.p1, 1)
     ve.tensor_tensor(hi, T.ps[:, 0:8], T.invd[:], mult).then_inc(S.p1, 1)
     ve.wait_ge(S.p1, 2)
-    ve.tensor_tensor(T.r1[:], T.sc[:], hi, sub).then_inc(S.p2, 1)
-    ve.tensor_tensor(mid, T.sc[:], hi, sub).then_inc(S.p2, 1)
-    ve.wait_ge(S.p2, 2)
-    ve.tensor_tensor(lo, T.r1[:], mid, sub).then_inc(S.p4, 1)
+    ve.tensor_tensor(mid, T.sc[:], hi, sub).then_inc(S.p4, 1)
 
     peers = _order(topo, T.cores, core)
     mask = topo.mask(core, peers[0])
@@ -124,27 +123,40 @@ def rank_program(g, core, T, topo):
     ve.wait_ge(S.t2, 1)
     ve.tensor_copy(T.rt2[0:K, :], T.pt2[0:K, 0:128]).then_inc(S.r2s, 1)
 
-    pe.wait_ge(S.r1s, 1)
-    pe.wait_ge(S.sl, 16 * NB)
-    for b in range(NB):
+    def spread(b):
         pm = T["pm%d" % b]
         pe.matmul(pm[:, 0:128], T.sel[0:K, 128 * b:128 * b + 128], T.rt1[0:K, :], True, True).then_inc(S["mb%d" % b], 1)
-        ve.wait_ge(S["mb%d" % b], 1)
-        ve.tensor_tensor(T.ysb[:, b::NB], T.xs[:, b::NB], pm[:, 0:128], sub).then_inc(S.yd, 1)
-    sy.wait_ge(S.yd, NB)
-    sy.dma_start(T.y[:], T.ysb[:]).then_inc(S.outy, 16)
 
-    pe.matmul(T.ps[:, 8:12], T.rt1[0:K, :], T.sel[0:K, 0:TK:128], True, True).then_inc(S.ms, 1)
+    def take(b):
+        ve.wait_ge(S["mb%d" % b], 1)
+        ve.tensor_tensor(T.ysb[:, b::NB], T.xs[:, b::NB], T["pm%d" % b][:, 0:128], sub).then_inc(S.yd, 1)
+
+    pe.wait_ge(S.r1s, 1)
+    pe.wait_ge(S.sl, 16 * NB)
+    pe.matmul(T.ps[:, 8:12], T.rt1[0:K, :], T.sel[0:K, 0:TK:128], True, True).then_inc(S.ms1, 1)
+    spread(0)
+    spread(1)
     pe.wait_ge(S.r2s, 1)
-    pe.matmul(T.ps[:, 12:16], T.rt2[0:K, :], T.sel[0:K, 0:TK:128], True, True).then_inc(S.ms, 1)
-    ve.wait_ge(S.ms, 2)
+    pe.matmul(T.pq[:, 0:4], T.rt2[0:K, :], T.sel[0:K, 0:TK:128], True, True).then_inc(S.ms2, 1)
+    spread(2)
+    spread(3)
+
+    ve.wait_ge(S.ms1, 1)
     ve.tensor_copy(T.msb[:], T.ps[:, 8:12]).then_inc(S.m1, 1)
-    sa.wait_ge(S.m1, 1)
-    sa.dma_start(T.m[:], T.msb[:]).then_inc(S.outm, 16)
+    take(0)
+    take(1)
     ve.wait_ge(S.m1, 1)
     ve.tensor_tensor(T.msq[:], T.ps[:, 8:12], T.msb[:], mult).then_inc(S.m2, 1)
+    take(2)
+    take(3)
+    ve.wait_ge(S.ms2, 1)
     ve.wait_ge(S.m2, 1)
-    ve.tensor_tensor(T.ssb[:], T.ps[:, 12:16], T.msq[:], sub).then_inc(S.m3, 1)
+    ve.tensor_tensor(T.ssb[:], T.pq[:, 0:4], T.msq[:], sub).then_inc(S.m3, 1)
+
+    sy.wait_ge(S.yd, NB)
+    sy.dma_start(T.y[:], T.ysb[:]).then_inc(S.outy, 16)
+    sa.wait_ge(S.m1, 1)
+    sa.dma_start(T.m[:], T.msb[:]).then_inc(S.outm, 16)
     sa.wait_ge(S.m3, 1)
     sa.dma_start(T.s[:], T.ssb[:]).then_inc(S.outs, 16)
 

from concourse.bass import DstId, RemoteDMATransfer
from concourse.mybir import dt, AluOpType

N = 9
TK = 512
D = 128 * N
NB = 4
NP = 2
SW = NP * 2 * NB
K = N * NP * NB

SCRATCH = {
    "xs": ("sbuf", [128, TK], "bfloat16"),
    "xq": ("sbuf", [128, TK], "float32"),
    "ysb": ("sbuf", [128, TK], "float32"),
    "R": ("sbuf", [128, N * SW], "bfloat16"),
    "onesb": ("sbuf", [128, 8], "bfloat16"),
    "onesf": ("sbuf", [128, 4], "float32"),
    "invd": ("sbuf", [128, 8], "float32"),
    "sc": ("sbuf", [128, 8], "float32"),
    "ia": ("sbuf", [128, 129], "bfloat16"),
    "ident": ("sbuf", [128, 128], "bfloat16"),
    "w": ("sbuf", [128, 896], "bfloat16"),
    "sel": ("sbuf", [128, TK], "bfloat16"),
    "rt1": ("sbuf", [128, 128], "bfloat16"),
    "rt2": ("sbuf", [128, 128], "bfloat16"),
    "msb": ("sbuf", [128, 4], "float32"),
    "msq": ("sbuf", [128, 4], "float32"),
    "ssb": ("sbuf", [128, 4], "float32"),
    "di": ("dram", [129, 128], "bfloat16"),
    "ps": ("psum", [128, 512], "float32"),
    "pq": ("psum", [128, 512], "float32"),
    "pt1": ("psum", [128, 512], "float32"),
    "pt2": ("psum", [128, 512], "float32"),
    "pm0": ("psum", [128, 512], "float32"),
    "pm1": ("psum", [128, 512], "float32"),
    "pm2": ("psum", [128, 512], "float32"),
    "pm3": ("psum", [128, 512], "float32"),
}
SEMAPHORES = ["ld", "c0", "c1", "c2", "id1", "id2", "sl", "sq0", "sq1", "sq2", "sq3", "st", "p1", "p4",
              "arr", "sent", "t1", "t2", "r1s", "r2s", "mb0", "mb1", "mb2", "mb3", "ms1", "ms2", "yd", "m1", "m2", "m3",
              "outy", "outm", "outs"]


def _order(topo, cores, core):
    mine = [c for c in cores if c == core or topo.same_plane(c, core)]
    other = [c for c in cores if c not in mine]
    i = mine.index(core)
    near = [mine[(i + s) % len(mine)] for s in range(1, len(mine))]
    mate = [c for c in other if topo.mates(core, c)]
    j = other.index(mate[0]) if mate else i
    far = [other[(j + 1 + k) % len(other)] for k in range(len(other))]
    return [c for c in far if c not in mate] + mate + near


def rank_program(g, core, T, topo):
    rank = T.rank_of(core)
    if rank is None:
        return
    S = T.sem
    pe, ve, sy, sa = g.tensor, g.vector, g.sync, g.scalar
    mult, sub = AluOpType.mult, AluOpType.subtract
    R = T.R
    slot = R[:, SW * rank:SW * rank + SW]
    hi, mid = [R[:, SW * rank + 8 * i:SW * rank + 8 * i + 8] for i in range(NP)]

    sy.dma_start(T.xs[:], T.x[:]).then_inc(S.ld, 16)

    ve.memset(T.ia[:, 0:1], 1.0).then_inc(S.c1, 1)
    ve.memset(T.ia[:, 1:129], 0.0).then_inc(S.c1, 1)
    ve.memset(T.onesb[:], 1.0).then_inc(S.c0, 1)
    ve.memset(T.onesf[:], 1.0).then_inc(S.c0, 1)
    ve.memset(T.invd[:], 1.0 / D).then_inc(S.c0, 1)
    ve.memset(T.w[0:K // NB, 0:384], 0.0).then_inc(S.c2, 1)
    ve.memset(T.w[0:K // NB, 384:512], 1.0).then_inc(S.c2, 1)
    ve.memset(T.w[0:K // NB, 512:896], 0.0).then_inc(S.c2, 1)
    sa.wait_ge(S.c1, 2)
    sa.dma_start(T.di[:], T.ia[:]).then_inc(S.id1, 16)
    sa.wait_ge(S.c2, 3)
    for b in range(NB):
        sa.dma_start(T.sel[b:K:NB, :], T.w[0:K // NB, 384 - 128 * b:896 - 128 * b]).then_inc(S.sl, 16)
    sa.wait_ge(S.id1, 16)
    sa.dma_start(T.ident[:], T.di[0:128, :]).then_inc(S.id2, 16)

    pe.wait_ge(S.ld, 16)
    pe.wait_ge(S.c0, 3)
    for b in range(NB):
        pe.matmul(T.ps[:, 2 * b:2 * b + 1], T.xs[:, b::NB], T.onesb[:, 0:1], True, True).then_inc(S.st, 1)
    ve.wait_ge(S.ld, 16)
    for b in range(NB):
        ve.tensor_tensor(T.xq[:, 128 * b:128 * b + 128], T.xs[:, b::NB], T.xs[:, b::NB], mult).then_inc(S["sq%d" % b], 1)
        pe.wait_ge(S["sq%d" % b], 1)
        pe.matmul(T.ps[:, 2 * b + 1:2 * b + 2], T.xq[:, 128 * b:128 * b + 128], T.onesf[:, 0:1],
                  True, True).then_inc(S.st, 1)

    ve.wait_ge(S.st, 8)
    ve.wait_ge(S.c0, 3)
    ve.tensor_tensor(T.sc[:], T.ps[:, 0:8], T.invd[:], mult).then_inc(S.p1, 1)
    ve.tensor_tensor(hi, T.ps[:, 0:8], T.invd[:], mult).then_inc(S.p1, 1)
    ve.wait_ge(S.p1, 2)
    ve.tensor_tensor(mid, T.sc[:], hi, sub).then_inc(S.p4, 1)

    peers = _order(topo, T.cores, core)
    mask = topo.mask(core, peers[0])
    for c in peers:
        mask &= topo.mask(core, c)
    eng = bin(mask).count("1")
    ids = []
    for c in peers:
        rid, pid = topo.addr(c, core)
        ids.append(DstId(rid=rid, pnc=pid))
    g.wait_ge(S.p4, 1)
    g.remote_dma_fused([RemoteDMATransfer(dst_ids=ids, dma_engine_mask=mask, remote_sem=S.arr,
                                          srcs=[slot], dsts=[slot for _ in peers])], local_sem=S.sent)

    pe.wait_ge(S.p4, 1)
    pe.wait_ge(S.id2, 16)
    pe.wait_ge(S.arr, eng * (N - 1))
    pe.matmul(T.pt1[0:K, 0:128], R[:, 0:2 * K:2], T.ident[:], True, True).then_inc(S.t1, 1)
    pe.matmul(T.pt2[0:K, 0:128], R[:, 1:2 * K:2], T.ident[:], True, True).then_inc(S.t2, 1)
    ve.wait_ge(S.t1, 1)
    ve.tensor_copy(T.rt1[0:K, :], T.pt1[0:K, 0:128]).then_inc(S.r1s, 1)
    ve.wait_ge(S.t2, 1)
    ve.tensor_copy(T.rt2[0:K, :], T.pt2[0:K, 0:128]).then_inc(S.r2s, 1)

    def spread(b):
        pm = T["pm%d" % b]
        pe.matmul(pm[:, 0:128], T.sel[0:K, 128 * b:128 * b + 128], T.rt1[0:K, :], True, True).then_inc(S["mb%d" % b], 1)

    def take(b):
        ve.wait_ge(S["mb%d" % b], 1)
        ve.tensor_tensor(T.ysb[:, b::NB], T.xs[:, b::NB], T["pm%d" % b][:, 0:128], sub).then_inc(S.yd, 1)

    pe.wait_ge(S.r1s, 1)
    pe.wait_ge(S.sl, 16 * NB)
    pe.matmul(T.ps[:, 8:12], T.rt1[0:K, :], T.sel[0:K, 0:TK:128], True, True).then_inc(S.ms1, 1)
    spread(0)
    spread(1)
    pe.wait_ge(S.r2s, 1)
    pe.matmul(T.pq[:, 0:4], T.rt2[0:K, :], T.sel[0:K, 0:TK:128], True, True).then_inc(S.ms2, 1)
    spread(2)
    spread(3)

    ve.wait_ge(S.ms1, 1)
    ve.tensor_copy(T.msb[:], T.ps[:, 8:12]).then_inc(S.m1, 1)
    take(0)
    take(1)
    ve.wait_ge(S.m1, 1)
    ve.tensor_tensor(T.msq[:], T.ps[:, 8:12], T.msb[:], mult).then_inc(S.m2, 1)
    take(2)
    take(3)
    ve.wait_ge(S.ms2, 1)
    ve.wait_ge(S.m2, 1)
    ve.tensor_tensor(T.ssb[:], T.pq[:, 0:4], T.msq[:], sub).then_inc(S.m3, 1)

    sy.wait_ge(S.yd, NB)
    sy.dma_start(T.y[:], T.ysb[:]).then_inc(S.outy, 16)
    sa.wait_ge(S.m1, 1)
    sa.dma_start(T.m[:], T.msb[:]).then_inc(S.outm, 16)
    sa.wait_ge(S.m3, 1)
    sa.dma_start(T.s[:], T.ssb[:]).then_inc(S.outs, 16)

    g.wait_ge(S.sent, eng)
    g.wait_ge(S.outy, 16)
    g.wait_ge(S.outm, 16)
    g.wait_ge(S.outs, 16)
